import numpy as np
import ml_dtypes


def mxq(x, axis, fmt="e4m3"):
    dtype, down = {"e4m3": (ml_dtypes.float8_e4m3fn, 7), "e5m2": (ml_dtypes.float8_e5m2, 14)}[fmt]
    v = np.moveaxis(np.asarray(x, np.float32).astype(ml_dtypes.bfloat16).astype(np.float64), axis, -1)
    blocks = v.reshape(v.shape[:-1] + (-1, 32))
    amax = np.abs(blocks).max(-1, keepdims=True)
    byte = np.maximum(np.where(amax > 0, np.frexp(amax)[1] - 1 + 127, 0) - down, 1)
    scale = np.exp2(byte - 127.0)
    codes = (blocks / scale).astype(np.float32).astype(dtype).astype(np.float64)
    return np.moveaxis((codes * scale).reshape(v.shape), -1, axis)


WIDE = False


def mx_kscale(k):
    if not WIDE:
        return np.ones(k)
    levels = np.array([10, -10, 5, -5, 0])
    if k % 512:
        return np.exp2(np.random.permutation(np.resize(levels, k // 32))).repeat(32)
    a = np.empty((k // 512, 16))
    for p in range(k // 512):
        a[p, :8] = np.random.permutation(np.resize(levels, 8))
        for g in range(8):
            far = levels[np.abs(levels - a[p, g]) >= 10]
            a[p, g + 8] = far[np.random.randint(len(far))]
    return np.exp2(a.ravel()).repeat(32)


def f64(x):
    return np.asarray(x).astype(np.float64)


def striped(idx):
    return np.tile(idx.reshape(-1, 16).T, (8, 1)).astype(np.uint16)


def unstriped(offs):
    return offs[:16].T.reshape(-1).astype(np.int64)


def pack_weight(w):
    k, n = w.shape
    w = f64(np.asarray(w, np.float32).astype(ml_dtypes.bfloat16)).reshape(k // 32, 32, n)
    amax = np.abs(w).max(1)
    byte = np.clip(np.where(amax > 0, np.frexp(amax)[1] - 1 + 127 - 7, 1), 1, 254)
    scaled = (w * np.exp2(127.0 - byte)[:, None, :]).reshape(k, n).astype(np.float32)
    words = np.ascontiguousarray(scaled.reshape(k // 512, 128, 4, n).transpose(0, 1, 3, 2)).astype(ml_dtypes.float8_e4m3fn).view(np.uint8)
    return words, np.ascontiguousarray(byte.astype(np.uint8).reshape(k // 512, 16, n))


def unpack_weight(words, scales):
    g, p, n, _ = words.shape
    vals = np.ascontiguousarray(words).view(ml_dtypes.float8_e4m3fn).astype(np.float64) * np.repeat(np.exp2(scales.astype(np.float64) - 127.0), 8, axis=1)[..., None]
    return vals.transpose(0, 1, 3, 2).reshape(g * 512, n)


K, T, S, V, H, N = 512, 4096, 1024, 512, 512, 256


def setup_inputs():
    n = np.random.standard_normal
    s = mx_kscale(K)[:, None]
    u = mx_kscale(H)
    packed_w2 = pack_weight(n((H, N)) / np.sqrt(3 * H) / u[:, None])
    packed_w3 = pack_weight(n((H, N)) / np.sqrt(3 * H) / u[:, None])
    packed_w4 = pack_weight(n((H, N)) / np.sqrt(3 * H) / u[:, None])
    return {
        "xT": (n((K, T)) * s).astype(np.float32),
        "w1": (n((K, H)) / np.sqrt(K) / s * u).astype(np.float32),
        "w2_words": packed_w2[0],
        "w2_scales": packed_w2[1],
        "w3_words": packed_w3[0],
        "w3_scales": packed_w3[1],
        "w4_words": packed_w4[0],
        "w4_scales": packed_w4[1],
        "offs": striped(np.random.permutation(T)[:S]),
        "pos1": striped(np.random.permutation(S)[:V]),
        "pos2": striped(np.random.permutation(S)[:V]),
        "pos3": striped(np.random.permutation(S)[:V]),
        "pos4": striped(np.random.permutation(S)[:V]),
    }


def reference(xT, w1, w2_words, w2_scales, w3_words, w3_scales, w4_words, w4_scales, offs, pos1, pos2, pos3, pos4):
    xq = mxq(f64(xT)[:, unstriped(offs)], 0, "e4m3")
    h = mxq(f64(w1), 0, "e4m3").T @ xq
    g0 = h[:, unstriped(pos1)]
    g1 = h[:, unstriped(pos2)]
    g2 = h[:, unstriped(pos3)]
    g3 = h[:, unstriped(pos4)]
    z1 = (g0 + g1 + g2 + g3) / 4
    z2 = np.maximum(np.maximum(np.maximum(g0, g1), g2), g3)
    z3 = np.minimum(np.minimum(np.minimum(g0, g1), g2), g3)
    return unpack_weight(w2_words, w2_scales).T @ mxq(z1, 0, "e4m3") + unpack_weight(w3_words, w3_scales).T @ mxq(z2, 0, "e4m3") + unpack_weight(w4_words, w4_scales).T @ mxq(z3, 0, "e4m3")

@@ -1,0 +1,142 @@
+from contextlib import ExitStack
+
+import concourse.mybir as mybir
+from concourse.masks import make_identity
+
+K, T, S, V, H, N = 512, 4096, 1024, 512, 512, 256
+D = 4
+FLOPS = 2 * K * H * S + 3 * 2 * H * N * V
+
+F32 = mybir.dt.float32
+BF16 = mybir.dt.bfloat16
+I32 = mybir.dt.int32
+U32 = mybir.dt.uint32
+U16 = mybir.dt.uint16
+U8 = mybir.dt.uint8
+FP8X4 = mybir.dt.float8_e4m3fn_x4
+MAX = mybir.AluOpType.max
+MIN = mybir.AluOpType.min
+COPY = mybir.ActivationFunctionType.Copy
+
+P = 128
+PACK = 4
+BANK = 512
+NODE_HALF = S // 2
+TGT_HALF = V // 2
+LIST_ROWS = 16
+
+
+def tile_picked_pna_none_e_kernel(tc, xT, w1, w2_words, w2_scales, w3_words, w3_scales, w4_words, w4_scales, offs, pos1, pos2, pos3, pos4, out):
+    nc = tc.nc
+    with ExitStack() as ctx:
+        keep = ctx.enter_context(tc.tile_pool(name="keep", bufs=1))
+        psum = ctx.enter_context(tc.psum_pool(name="psum", bufs=1))
+
+        def quantize(values, name):
+            width = values.shape[1] // PACK
+            codes = keep.tile([P, width], U32, name=name + "_codes", align_bytes=64)
+            scales = keep.tile([P, width], U8, name=name + "_scales", align_bytes=64)
+            nc.vector.quantize_mx(out=codes[:].bitcast(FP8X4), scales=scales[:], in_=values)
+            return codes, scales
+
+        offs_sb = keep.tile([P, S // LIST_ROWS], U16, name="offs_sb")
+        x_rows = xT.rearrange("(p j) w -> p j w", j=PACK)
+        planes = [keep.tile([P, T], F32, name="x_plane%d" % j) for j in range(PACK)]
+        for j in range(PACK):
+            nc.sync.dma_start(planes[j][:], x_rows[:, j, :])
+            if j == 0:
+                nc.sync.dma_start(offs_sb[:], offs)
+        w1_rows = w1.rearrange("(p j) c -> p j c", j=PACK)
+        w1_raw = [keep.tile([P, PACK, H // 2], F32, name="w1_raw%d" % c) for c in range(2)]
+        for c in range(2):
+            nc.sync.dma_start(w1_raw[c][:], w1_rows[:, :, c * (H // 2):(c + 1) * (H // 2)])
+        pos_sb = [keep.tile([P, V // LIST_ROWS], U16, name="pos_sb%d" % d) for d in range(D)]
+        for d, pos in enumerate((pos1, pos2, pos3, pos4)):
+            nc.sync.dma_start(pos_sb[d][:], pos)
+        w_codes = [keep.tile([P, N], U32, name="w_codes%d" % a, align_bytes=64) for a in range(3)]
+        for a, words in enumerate((w2_words, w3_words, w4_words)):
+            nc.sync.dma_start(w_codes[a][:].bitcast(I32), words[0].rearrange("p n t -> p (n t)").bitcast(I32))
+        w_scales = keep.tile([P, 3 * N], U8, name="w_scales", align_bytes=64)
+        nc.gpsimd.memset(w_scales[:], 0)
+        for a, scale_rows in enumerate((w2_scales, w3_scales, w4_scales)):
+            for q in range(4):
+                nc.sync.dma_start(w_scales[32 * q:32 * q + 4, a * N:(a + 1) * N].bitcast(I32), scale_rows[0, 4 * q:4 * q + 4, :].bitcast(I32))
+        ident = keep.tile([P, P], F32, name="ident")
+        make_identity(nc, ident[:])
+
+        picked = [keep.tile([P, NODE_HALF, PACK], BF16, name="picked%d" % n, align_bytes=64) for n in range(2)]
+        x_q = []
+        cols = NODE_HALF // LIST_ROWS
+        for j in range(PACK):
+            for n in range(2):
+                nc.vector.tensor_copy(picked[n][:, :, j], planes[j][:].indirect(offs_sb[:, n * cols:(n + 1) * cols]))
+                if j == PACK - 1:
+                    x_q.append(quantize(picked[n][:].rearrange("p n j -> p (n j)"), "x%d" % n))
+
+        w1_bf = keep.tile([P, PACK, P, PACK], BF16, name="w1_bf", align_bytes=64)
+        for c in range(2):
+            nc.scalar.copy(w1_bf[:, :, c * (P // 2):(c + 1) * (P // 2), :].rearrange("p t m j -> p m j t"),
+                           w1_raw[c][:].rearrange("p j (m t) -> p m j t", t=PACK))
+        w1_q = [quantize(w1_bf[:, t].rearrange("p m j -> p (m j)"), "w1_%d" % t) for t in range(PACK)]
+
+        h = [keep.tile([P, S], F32, name="h%d" % t) for t in range(PACK)]
+        for t in range(PACK):
+            for n in range(2):
+                acc = psum.tile([P, BANK], F32, name="acc", tag="mx%d" % ((2 * t + n) % 4))
+                nc.tensor.matmul_mx(acc[:], lhsT=w1_q[t][0][:].bitcast(FP8X4), lhsT_scale=w1_q[t][1][:],
+                                    rhs=x_q[n][0][:].bitcast(FP8X4), rhs_scale=x_q[n][1][:], start=True, stop=True)
+                dst = h[t][:, n * NODE_HALF:(n + 1) * NODE_HALF]
+                if t == 0 and n == 1:
+                    nc.vector.tensor_copy(dst, acc[:])
+                else:
+                    nc.scalar.copy(dst, acc[:])
+
+        hi = keep.tile([P, 2, 2, V * 2], BF16, name="hi", align_bytes=64)
+        lo = keep.tile([P, 2, 2, V * 2], BF16, name="lo", align_bytes=64)
+        back = [psum.tile([P, 2, TGT_HALF], F32, name="back%d" % v) for v in range(2)]
+        for u in range(2):
+            g = [keep.tile([P, 2, V], F32, name="g%d_%d" % (u, d)) for d in range(D)]
+            sums = [psum.tile([P, 2, 2, P], F32, name="sums", tag="sums%d" % v) for v in range(2)]
+            for e in range(2):
+                for d in range(D):
+                    nc.vector.tensor_copy(g[d][:, e, :], h[2 * u + e][:].indirect(pos_sb[d][:]))
+                for b in range(V // P):
+                    for d in range(D):
+                        nc.tensor.matmul(sums[b // 2][:, b % 2, e, :], lhsT=g[d][:, e, b * P:(b + 1) * P], rhs=ident[:],
+                                         is_transpose=True, start=(d == 0), stop=(d == D - 1))
+            rounded = keep.tile([P, D, V, 2], BF16, name="rounded%d" % u, align_bytes=64)
+            for d in range(D):
+                nc.scalar.copy(rounded[:, d], g[d][:].rearrange("p e v -> p v e"))
+            for v in range(2):
+                mean_t = keep.tile([P, 2, P, 2], BF16, name="mean_t%d_%d" % (u, v), align_bytes=64)
+                nc.scalar.activation(mean_t[:], sums[v][:].rearrange("p b e c -> p b c e"), COPY, scale=1.0 / D)
+                mean_words = mean_t[:].rearrange("p b c e -> p (b c e)").bitcast(F32)
+                for b in range(2):
+                    nc.tensor.transpose(back[v][:, u, b * P:(b + 1) * P], mean_words[:, b * P:(b + 1) * P], ident[:])
+            first = rounded[:, 0:2].rearrange("p d v e -> p d (v e)")
+            second = rounded[:, 2:4].rearrange("p d v e -> p d (v e)")
+            nc.vector.tensor_tensor(hi[:, :, u, :], first, second, MAX)
+            nc.vector.tensor_tensor(lo[:, :, u, :], first, second, MIN)
+
+        for v in range(2):
+            z = [keep.tile([P, TGT_HALF, 2, 2], BF16, name="z%d_%d" % (a, v), align_bytes=64) for a in range(3)]
+            nc.scalar.copy(z[0][:].rearrange("p v u e -> p (v u e)").bitcast(F32).rearrange("p (v u) -> p v u", u=2),
+                           back[v][:].rearrange("p u v -> p v u"))
+            span = slice(v * TGT_HALF * 2, (v + 1) * TGT_HALF * 2)
+            for a, pairs, op in ((1, hi, MAX), (2, lo, MIN)):
+                nc.vector.tensor_tensor(z[a][:], pairs[:, 0, :, span].rearrange("p u (v e) -> p v u e", e=2),
+                                        pairs[:, 1, :, span].rearrange("p u (v e) -> p v u e", e=2), op)
+            z_q = [quantize(z[a][:].rearrange("p v u e -> p (v u e)"), "z%d_%d" % (a, v)) for a in range(3)]
+            for m in range(N // P):
+                acc = psum.tile([P, TGT_HALF], F32, name="acc", tag="mx%d" % (2 * v + m))
+                for a in range(3):
+                    nc.tensor.matmul_mx(acc[:], lhsT=w_codes[a][:, m * P:(m + 1) * P].bitcast(FP8X4),
+                                        lhsT_scale=w_scales[:, a * N + m * P:a * N + (m + 1) * P],
+                                        rhs=z_q[a][0][:].bitcast(FP8X4), rhs_scale=z_q[a][1][:],
+                                        start=(a == 0), stop=(a == 2))
+                result = keep.tile([P, TGT_HALF], F32, name="result%d_%d" % (v, m))
+                if v == 1 and m == 1:
+                    nc.vector.tensor_copy(result[:], acc[:])
+                else:
+                    nc.scalar.copy(result[:], acc[:])
+                nc.sync.dma_start(out[m * P:(m + 1) * P, v * TGT_HALF:(v + 1) * TGT_HALF], result[:])

@@ -24,6 +24,7 @@ BANK = 512
 NODE_HALF = S // 2
 TGT_HALF = V // 2
 LIST_ROWS = 16
+W1_SPLIT = 64
 
 
 def tile_picked_pna_none_e_kernel(tc, xT, w1, w2_words, w2_scales, w3_words, w3_scales, w4_words, w4_scales, offs, pos1, pos2, pos3, pos4, out):
@@ -47,9 +48,10 @@ def tile_picked_pna_none_e_kernel(tc, xT, w1, w2_words, w2_scales, w3_words, w3_
             if j == 0:
                 nc.sync.dma_start(offs_sb[:], offs)
         w1_rows = w1.rearrange("(p j) c -> p j c", j=PACK)
-        w1_raw = [keep.tile([P, PACK, H // 2], F32, name="w1_raw%d" % c) for c in range(2)]
-        for c in range(2):
-            nc.sync.dma_start(w1_raw[c][:], w1_rows[:, :, c * (H // 2):(c + 1) * (H // 2)])
+        w1_spans = ((0, W1_SPLIT), (W1_SPLIT, P))
+        w1_raw = [keep.tile([P, PACK, PACK * (m1 - m0)], F32, name="w1_raw%d" % m0) for m0, m1 in w1_spans]
+        for raw, (m0, m1) in zip(w1_raw, w1_spans):
+            nc.sync.dma_start(raw[:], w1_rows[:, :, PACK * m0:PACK * m1])
         pos_sb = [keep.tile([P, V // LIST_ROWS], U16, name="pos_sb%d" % d) for d in range(D)]
         for d, pos in enumerate((pos1, pos2, pos3, pos4)):
             nc.sync.dma_start(pos_sb[d][:], pos)
@@ -65,68 +67,92 @@ def tile_picked_pna_none_e_kernel(tc, xT, w1, w2_words, w2_scales, w3_words, w3_
         make_identity(nc, ident[:])
 
         picked = [keep.tile([P, NODE_HALF, PACK], BF16, name="picked%d" % n, align_bytes=64) for n in range(2)]
-        x_q = []
         cols = NODE_HALF // LIST_ROWS
         for j in range(PACK):
             for n in range(2):
                 nc.vector.tensor_copy(picked[n][:, :, j], planes[j][:].indirect(offs_sb[:, n * cols:(n + 1) * cols]))
-                if j == PACK - 1:
-                    x_q.append(quantize(picked[n][:].rearrange("p n j -> p (n j)"), "x%d" % n))
+                if j == PACK - 1 and n == 0:
+                    xa_codes, xa_scales = quantize(picked[0][:].rearrange("p n j -> p (n j)"), "xa")
 
-        w1_bf = keep.tile([P, PACK, P, PACK], BF16, name="w1_bf", align_bytes=64)
-        for c in range(2):
-            nc.scalar.copy(w1_bf[:, :, c * (P // 2):(c + 1) * (P // 2), :].rearrange("p t m j -> p m j t"),
-                           w1_raw[c][:].rearrange("p j (m t) -> p m j t", t=PACK))
-        w1_q = [quantize(w1_bf[:, t].rearrange("p m j -> p (m j)"), "w1_%d" % t) for t in range(PACK)]
+        w1_first = keep.tile([P, P, PACK], BF16, name="w1_first", tag="w1_then_xb", align_bytes=64)
+        w1_rest = keep.tile([P, PACK - 1, P, PACK], BF16, name="w1_rest", align_bytes=64)
+        for raw, (m0, m1) in zip(w1_raw, w1_spans):
+            dealt = raw[:].rearrange("p j (m t) -> p m j t", t=PACK)
+            nc.scalar.copy(w1_first[:, m0:m1, :], dealt[:, :, :, 0])
+            nc.scalar.copy(w1_rest[:, :, m0:m1, :].rearrange("p t m j -> p m j t"), dealt[:, :, :, 1:PACK])
+        w10_codes, w10_scales = quantize(w1_first[:].rearrange("p m j -> p (m j)"), "w1_0")
+        xb_codes = keep.tile([P, NODE_HALF], U32, name="xb_codes", tag="w1_then_xb", align_bytes=64)
+        xb_scales = keep.tile([P, NODE_HALF], U8, name="xb_scales", align_bytes=64)
+        quarter = NODE_HALF // 2
+        for r in range(2):
+            span = slice(r * quarter, (r + 1) * quarter)
+            nc.vector.quantize_mx(out=xb_codes[:, span].bitcast(FP8X4), scales=xb_scales[:, span],
+                                  in_=picked[1][:, span, :].rearrange("p n j -> p (n j)"))
+        w1_q = [(w10_codes[:], w10_scales[:])]
 
         h = [keep.tile([P, S], F32, name="h%d" % t) for t in range(PACK)]
-        for t in range(PACK):
-            for n in range(2):
-                acc = psum.tile([P, BANK], F32, name="acc", tag="mx%d" % ((2 * t + n) % 4))
-                nc.tensor.matmul_mx(acc[:], lhsT=w1_q[t][0][:].bitcast(FP8X4), lhsT_scale=w1_q[t][1][:],
-                                    rhs=x_q[n][0][:].bitcast(FP8X4), rhs_scale=x_q[n][1][:], start=True, stop=True)
-                dst = h[t][:, n * NODE_HALF:(n + 1) * NODE_HALF]
-                if t == 0 and n == 1:
-                    nc.vector.tensor_copy(dst, acc[:])
-                else:
-                    nc.scalar.copy(dst, acc[:])
+        pieces = [(0, 0, NODE_HALF), (0, NODE_HALF, quarter), (0, NODE_HALF + quarter, quarter),
+                  (1, 0, NODE_HALF), (1, NODE_HALF, NODE_HALF),
+                  (2, 0, NODE_HALF), (3, 0, NODE_HALF), (2, NODE_HALF, NODE_HALF), (3, NODE_HALF, NODE_HALF)]
+        banks = ["mx0", "mx1", "mx2", "mx3", "back0", "back1", "mx0", "sums0", "sums1"]
+        for bank, (t, n0, width) in zip(banks, pieces):
+            if t == 1 and n0 == 0:
+                codes, scales = quantize(w1_rest[:, 0].rearrange("p m j -> p (m j)"), "w1_1")
+                w1_q.append((codes[:], scales[:]))
+                codes, scales = quantize(w1_rest[:, 1:3].rearrange("p t m j -> p (t m j)"), "w1_23")
+                w1_q.extend([(codes[:, i * P:(i + 1) * P], scales[:, i * P:(i + 1) * P]) for i in range(2)])
+            acc = psum.tile([P, width], F32, name="acc", tag=bank)
+            codes, scales = (xa_codes, xa_scales) if n0 < NODE_HALF else (xb_codes, xb_scales)
+            span = slice(n0 % NODE_HALF, n0 % NODE_HALF + width)
+            nc.tensor.matmul_mx(acc[:], lhsT=w1_q[t][0].bitcast(FP8X4), lhsT_scale=w1_q[t][1],
+                                rhs=codes[:, span].bitcast(FP8X4), rhs_scale=scales[:, span], start=True, stop=True)
+            if n0 == NODE_HALF + quarter:
+                nc.vector.tensor_copy(h[t][:, n0:n0 + width], acc[:])
+            else:
+                nc.scalar.copy(h[t][:, n0:n0 + width], acc[:])
 
-        hi = keep.tile([P, 2, 2, V * 2], BF16, name="hi", align_bytes=64)
-        lo = keep.tile([P, 2, 2, V * 2], BF16, name="lo", align_bytes=64)
-        back = [psum.tile([P, 2, TGT_HALF], F32, name="back%d" % v) for v in range(2)]
+        rounded = [keep.tile([P, V, 2, 2], BF16, name="rounded%d" % d, align_bytes=64) for d in range(D)]
+        back = [psum.tile([P, 2, TGT_HALF], F32, name="back", tag="back%d" % v) for v in range(2)]
         for u in range(2):
             g = [keep.tile([P, 2, V], F32, name="g%d_%d" % (u, d)) for d in range(D)]
-            sums = [psum.tile([P, 2, 2, P], F32, name="sums", tag="sums%d" % v) for v in range(2)]
-            for e in range(2):
-                for d in range(D):
-                    nc.vector.tensor_copy(g[d][:, e, :], h[2 * u + e][:].indirect(pos_sb[d][:]))
+            sums = [psum.tile([P, 2, 2, P], F32, name="sums", tag=("sums%d" % v, "mx%d" % (2 + v))[u]) for v in range(2)]
+            if u == 0:
+                order = [(d, e) for e in range(2) for d in range(D)]
+            else:
+                order = [(d, e) for d in range(D) for e in range(2)]
+            for i, (d, e) in enumerate(order):
+                nc.vector.tensor_copy(g[d][:, e, :], h[2 * u + e][:].indirect(pos_sb[d][:]))
                 for b in range(V // P):
-                    for d in range(D):
-                        nc.tensor.matmul(sums[b // 2][:, b % 2, e, :], lhsT=g[d][:, e, b * P:(b + 1) * P], rhs=ident[:],
-                                         is_transpose=True, start=(d == 0), stop=(d == D - 1))
-            rounded = keep.tile([P, D, V, 2], BF16, name="rounded%d" % u, align_bytes=64)
-            for d in range(D):
-                nc.scalar.copy(rounded[:, d], g[d][:].rearrange("p e v -> p v e"))
+                    nc.tensor.matmul(sums[b // 2][:, b % 2, e, :], lhsT=g[d][:, e, b * P:(b + 1) * P], rhs=ident[:],
+                                     is_transpose=True, start=(i == 0 and b % 2 == 0), stop=(i == len(order) - 1 and b % 2 == 1))
+            for d in range(D - u):
+                nc.scalar.copy(rounded[d][:, :, u, :], g[d][:].rearrange("p e v -> p v e"))
             for v in range(2):
                 mean_t = keep.tile([P, 2, P, 2], BF16, name="mean_t%d_%d" % (u, v), align_bytes=64)
                 nc.scalar.activation(mean_t[:], sums[v][:].rearrange("p b e c -> p b c e"), COPY, scale=1.0 / D)
                 mean_words = mean_t[:].rearrange("p b c e -> p (b c e)").bitcast(F32)
                 for b in range(2):
                     nc.tensor.transpose(back[v][:, u, b * P:(b + 1) * P], mean_words[:, b * P:(b + 1) * P], ident[:])
-            first = rounded[:, 0:2].rearrange("p d v e -> p d (v e)")
-            second = rounded[:, 2:4].rearrange("p d v e -> p d (v e)")
-            nc.vector.tensor_tensor(hi[:, :, u, :], first, second, MAX)
-            nc.vector.tensor_tensor(lo[:, :, u, :], first, second, MIN)
+            if u == 1:
+                nc.scalar.copy(rounded[D - 1][:, :, u, :], g[D - 1][:].rearrange("p e v -> p v e"))
+
+        flat = [r[:].rearrange("p v u e -> p (v u e)") for r in rounded]
+        hi, lo = flat[0], flat[0]
+        for d in range(1, D - 1):
+            hi_next = keep.tile([P, V * PACK], BF16, name="hi%d" % d, align_bytes=64)
+            lo_next = keep.tile([P, V * PACK], BF16, name="lo%d" % d, align_bytes=64)
+            nc.vector.tensor_tensor(hi_next[:], hi, flat[d], MAX)
+            nc.vector.tensor_tensor(lo_next[:], lo, flat[d], MIN)
+            hi, lo = hi_next[:], lo_next[:]
 
         for v in range(2):
-            z = [keep.tile([P, TGT_HALF, 2, 2], BF16, name="z%d_%d" % (a, v), align_bytes=64) for a in range(3)]
-            nc.scalar.copy(z[0][:].rearrange("p v u e -> p (v u e)").bitcast(F32).rearrange("p (v u) -> p v u", u=2),
-                           back[v][:].rearrange("p u v -> p v u"))
-            span = slice(v * TGT_HALF * 2, (v + 1) * TGT_HALF * 2)
-            for a, pairs, op in ((1, hi, MAX), (2, lo, MIN)):
-                nc.vector.tensor_tensor(z[a][:], pairs[:, 0, :, span].rearrange("p u (v e) -> p v u e", e=2),
-                                        pairs[:, 1, :, span].rearrange("p u (v e) -> p v u e", e=2), op)
-            z_q = [quantize(z[a][:].rearrange("p v u e -> p (v u e)"), "z%d_%d" % (a, v)) for a in range(3)]
+            z = [keep.tile([P, TGT_HALF * PACK], BF16, name="z%d_%d" % (a, v), align_bytes=64) for a in range(3)]
+            nc.scalar.copy(z[0][:].bitcast(F32).rearrange("p (v u) -> p v u", u=2), back[v][:].rearrange("p u v -> p v u"))
+            span = slice(v * TGT_HALF * PACK, (v + 1) * TGT_HALF * PACK)
+            nc.vector.tensor_tensor(z[1][:], hi[:, span], flat[D - 1][:, span], MAX)
+            z_q = [quantize(z[0][:], "z0_%d" % v)]
+            nc.vector.tensor_tensor(z[2][:], lo[:, span], flat[D - 1][:, span], MIN)
+            z_q.extend([quantize(z[a][:], "z%d_%d" % (a, v)) for a in (1, 2)])
             for m in range(N // P):
                 acc = psum.tile([P, TGT_HALF], F32, name="acc", tag="mx%d" % (2 * v + m))
                 for a in range(3):
@@ -139,4 +165,5 @@ def tile_picked_pna_none_e_kernel(tc, xT, w1, w2_words, w2_scales, w3_words, w3_
                     nc.vector.tensor_copy(result[:], acc[:])
                 else:
                     nc.scalar.copy(result[:], acc[:])
-                nc.sync.dma_start(out[m * P:(m + 1) * P, v * TGT_HALF:(v + 1) * TGT_HALF], result[:])
+                queue = nc.scalar if (v == 1 and m == 0) else nc.sync
+                queue.dma_start(out[m * P:(m + 1) * P, v * TGT_HALF:(v + 1) * TGT_HALF], result[:])

@@ -90,53 +90,70 @@ def tile_picked_pna_none_e_kernel(tc, xT, w1, w2_words, w2_scales, w3_words, w3_
                                   in_=picked[1][:, span, :].rearrange("p n j -> p (n j)"))
         w1_q = [(w10_codes[:], w10_scales[:])]
 
-        h = [keep.tile([P, S], F32, name="h%d" % t) for t in range(PACK)]
-        pieces = [(0, 0, NODE_HALF), (0, NODE_HALF, quarter), (0, NODE_HALF + quarter, quarter),
-                  (1, 0, NODE_HALF), (1, NODE_HALF, NODE_HALF),
-                  (2, 0, NODE_HALF), (3, 0, NODE_HALF), (2, NODE_HALF, NODE_HALF), (3, NODE_HALF, NODE_HALF)]
+        h0 = keep.tile([P, S], F32, name="h0")
+        h1 = keep.tile([P, S], F32, name="h1")
+        h23 = keep.tile([P, 2, S], F32, name="h23")
+        h = [h0[:], h1[:], h23[:, 0, :], h23[:, 1, :]]
+        pieces = [((0,), 0, NODE_HALF), ((0,), NODE_HALF, quarter), ((0,), NODE_HALF + quarter, quarter),
+                  ((1,), 0, NODE_HALF), ((1,), NODE_HALF, NODE_HALF), ((2,), 0, NODE_HALF), ((3,), 0, NODE_HALF),
+                  ((2, 3), NODE_HALF, quarter), ((2, 3), NODE_HALF + quarter, quarter)]
         banks = ["mx0", "mx1", "mx2", "mx3", "back0", "back1", "mx0", "sums0", "sums1"]
-        for bank, (t, n0, width) in zip(banks, pieces):
-            if t == 1 and n0 == 0:
+        for bank, (ts, n0, width) in zip(banks, pieces):
+            if ts == (1,) and n0 == 0:
                 codes, scales = quantize(w1_rest[:, 0].rearrange("p m j -> p (m j)"), "w1_1")
                 w1_q.append((codes[:], scales[:]))
                 codes, scales = quantize(w1_rest[:, 1:3].rearrange("p t m j -> p (t m j)"), "w1_23")
                 w1_q.extend([(codes[:, i * P:(i + 1) * P], scales[:, i * P:(i + 1) * P]) for i in range(2)])
-            acc = psum.tile([P, width], F32, name="acc", tag=bank)
+            acc = psum.tile([P, len(ts), width], F32, name="acc", tag=bank)
             codes, scales = (xa_codes, xa_scales) if n0 < NODE_HALF else (xb_codes, xb_scales)
             span = slice(n0 % NODE_HALF, n0 % NODE_HALF + width)
-            nc.tensor.matmul_mx(acc[:], lhsT=w1_q[t][0].bitcast(FP8X4), lhsT_scale=w1_q[t][1],
-                                rhs=codes[:, span].bitcast(FP8X4), rhs_scale=scales[:, span], start=True, stop=True)
-            if n0 == NODE_HALF + quarter:
-                nc.vector.tensor_copy(h[t][:, n0:n0 + width], acc[:])
+            for i, t in enumerate(ts):
+                nc.tensor.matmul_mx(acc[:, i, :], lhsT=w1_q[t][0].bitcast(FP8X4), lhsT_scale=w1_q[t][1],
+                                    rhs=codes[:, span].bitcast(FP8X4), rhs_scale=scales[:, span], start=True, stop=True)
+            if len(ts) == 2:
+                nc.scalar.copy(h23[:, :, n0:n0 + width], acc[:])
+            elif n0 == NODE_HALF + quarter:
+                nc.vector.tensor_copy(h[ts[0]][:, n0:n0 + width], acc[:, 0, :])
             else:
-                nc.scalar.copy(h[t][:, n0:n0 + width], acc[:])
+                nc.scalar.copy(h[ts[0]][:, n0:n0 + width], acc[:, 0, :])
 
-        rounded = [keep.tile([P, V, 2, 2], BF16, name="rounded%d" % d, align_bytes=64) for d in range(D)]
+        g = [keep.tile([P, PACK, V], F32, name="g%d" % d) for d in range(D)]
+        rounded = [keep.tile([P, V, PACK], BF16, name="rounded%d" % d, align_bytes=64) for d in range(D - 1)]
         back = [psum.tile([P, 2, TGT_HALF], F32, name="back", tag="back%d" % v) for v in range(2)]
+        mean = [keep.tile([P, TGT_HALF * PACK], BF16, name="mean%d" % v, align_bytes=64) for v in range(2)]
+
+        def round_and_weave(dst, d, span):
+            nc.scalar.copy(dst.rearrange("p (c i) t -> p c t i", i=4),
+                           g[d][:, :, span].rearrange("p t (c i) -> p c t i", i=4))
+
         for u in range(2):
-            g = [keep.tile([P, 2, V], F32, name="g%d_%d" % (u, d)) for d in range(D)]
-            sums = [psum.tile([P, 2, 2, P], F32, name="sums", tag=("sums%d" % v, "mx%d" % (2 + v))[u]) for v in range(2)]
+            sums = [psum.tile([P, 2, 2, P], F32, name="sums", tag=("mx%d" % (1 + v), "sums%d" % v)[u]) for v in range(2)]
             if u == 0:
                 order = [(d, e) for e in range(2) for d in range(D)]
             else:
                 order = [(d, e) for d in range(D) for e in range(2)]
             for i, (d, e) in enumerate(order):
-                nc.vector.tensor_copy(g[d][:, e, :], h[2 * u + e][:].indirect(pos_sb[d][:]))
+                t = 2 * u + e
+                nc.vector.tensor_copy(g[d][:, t, :], h[t].indirect(pos_sb[d][:]))
                 for b in range(V // P):
-                    nc.tensor.matmul(sums[b // 2][:, b % 2, e, :], lhsT=g[d][:, e, b * P:(b + 1) * P], rhs=ident[:],
+                    nc.tensor.matmul(sums[b // 2][:, b % 2, e, :], lhsT=g[d][:, t, b * P:(b + 1) * P], rhs=ident[:],
                                      is_transpose=True, start=(i == 0 and b % 2 == 0), stop=(i == len(order) - 1 and b % 2 == 1))
-            for d in range(D - u):
-                nc.scalar.copy(rounded[d][:, :, u, :], g[d][:].rearrange("p e v -> p v e"))
+                if t == PACK - 1 and d < D - 1:
+                    round_and_weave(rounded[d][:], d, slice(0, V))
             for v in range(2):
-                mean_t = keep.tile([P, 2, P, 2], BF16, name="mean_t%d_%d" % (u, v), align_bytes=64)
+                mean_t = keep.tile([P, 2, P, 2], BF16, name="mean_t", tag="mean_t%d_%d" % (u, v), align_bytes=64)
                 nc.scalar.activation(mean_t[:], sums[v][:].rearrange("p b e c -> p b c e"), COPY, scale=1.0 / D)
                 mean_words = mean_t[:].rearrange("p b c e -> p (b c e)").bitcast(F32)
                 for b in range(2):
                     nc.tensor.transpose(back[v][:, u, b * P:(b + 1) * P], mean_words[:, b * P:(b + 1) * P], ident[:])
-            if u == 1:
-                nc.scalar.copy(rounded[D - 1][:, :, u, :], g[D - 1][:].rearrange("p e v -> p v e"))
+        last = []
+        for v in range(2):
+            tile = keep.tile([P, TGT_HALF, PACK], BF16, name="last", tag="mean_t1_%d" % v, align_bytes=64)
+            round_and_weave(tile[:], D - 1, slice(v * TGT_HALF, (v + 1) * TGT_HALF))
+            last.append(tile[:].rearrange("p v t -> p (v t)"))
+            nc.scalar.copy(mean[v][:].bitcast(F32).rearrange("p (v u) -> p v u", u=2), back[v][:].rearrange("p u v -> p v u"))
 
-        flat = [r[:].rearrange("p v u e -> p (v u e)") for r in rounded]
+        flat = [r[:].rearrange("p v t -> p (v t)") for r in rounded]
         hi, lo = flat[0], flat[0]
         for d in range(1, D - 1):
             hi_next = keep.tile([P, V * PACK], BF16, name="hi%d" % d, align_bytes=64)
@@ -145,25 +162,35 @@ def tile_picked_pna_none_e_kernel(tc, xT, w1, w2_words, w2_scales, w3_words, w3_
             nc.vector.tensor_tensor(lo_next[:], lo, flat[d], MIN)
             hi, lo = hi_next[:], lo_next[:]
 
+        out_rows = out.rearrange("(m p) v -> p m v", p=P)
+        free_banks = ["mx0", "mx3", "mx1", "mx2", "sums0", "sums1"]
         for v in range(2):
-            z = [keep.tile([P, TGT_HALF * PACK], BF16, name="z%d_%d" % (a, v), align_bytes=64) for a in range(3)]
-            nc.scalar.copy(z[0][:].bitcast(F32).rearrange("p (v u) -> p v u", u=2), back[v][:].rearrange("p u v -> p v u"))
-            span = slice(v * TGT_HALF * PACK, (v + 1) * TGT_HALF * PACK)
-            nc.vector.tensor_tensor(z[1][:], hi[:, span], flat[D - 1][:, span], MAX)
-            z_q = [quantize(z[0][:], "z0_%d" % v)]
-            nc.vector.tensor_tensor(z[2][:], lo[:, span], flat[D - 1][:, span], MIN)
-            z_q.extend([quantize(z[a][:], "z%d_%d" % (a, v)) for a in (1, 2)])
-            for m in range(N // P):
-                acc = psum.tile([P, TGT_HALF], F32, name="acc", tag="mx%d" % (2 * v + m))
-                for a in range(3):
-                    nc.tensor.matmul_mx(acc[:], lhsT=w_codes[a][:, m * P:(m + 1) * P].bitcast(FP8X4),
-                                        lhsT_scale=w_scales[:, a * N + m * P:a * N + (m + 1) * P],
-                                        rhs=z_q[a][0][:].bitcast(FP8X4), rhs_scale=z_q[a][1][:],
-                                        start=(a == 0), stop=(a == 2))
-                result = keep.tile([P, TGT_HALF], F32, name="result%d_%d" % (v, m))
-                if v == 1 and m == 1:
-                    nc.vector.tensor_copy(result[:], acc[:])
-                else:
-                    nc.scalar.copy(result[:], acc[:])
-                queue = nc.scalar if (v == 1 and m == 0) else nc.sync
-                queue.dma_start(out[m * P:(m + 1) * P, v * TGT_HALF:(v + 1) * TGT_HALF], result[:])
+            v0 = v * TGT_HALF
+            largest = keep.tile([P, TGT_HALF * PACK], BF16, name="largest%d" % v, align_bytes=64)
+            nc.vector.tensor_tensor(largest[:], hi[:, v0 * PACK:(v0 + TGT_HALF) * PACK], last[v], MAX)
+            z1 = quantize(mean[v][:], "z1_%d" % v)
+            width = TGT_HALF // (v + 1)
+            starts = range(0, TGT_HALF, width)
+            smallest = [keep.tile([P, width * PACK], BF16, name="smallest%d_%d" % (v, c0), align_bytes=64) for c0 in starts]
+            z2 = None
+            for tile, c0 in zip(smallest, starts):
+                span = slice((v0 + c0) * PACK, (v0 + c0 + width) * PACK)
+                nc.vector.tensor_tensor(tile[:], lo[:, span], last[v][:, c0 * PACK:(c0 + width) * PACK], MIN)
+                if c0 == 0:
+                    z2 = quantize(largest[:], "z2_%d" % v)
+            for tile, c0 in zip(smallest, starts):
+                z3 = quantize(tile[:], "z3_%d_%d" % (v, c0))
+                moving = [(z1[0][:, c0:c0 + width], z1[1][:, c0:c0 + width]), (z2[0][:, c0:c0 + width], z2[1][:, c0:c0 + width]), (z3[0][:], z3[1][:])]
+                result = keep.tile([P, N // P, width], F32, name="result%d_%d" % (v, c0))
+                for m in range(N // P):
+                    acc = psum.tile([P, width], F32, name="acc", tag=free_banks.pop(0))
+                    for a in range(3):
+                        nc.tensor.matmul_mx(acc[:], lhsT=w_codes[a][:, m * P:(m + 1) * P].bitcast(FP8X4),
+                                            lhsT_scale=w_scales[:, a * N + m * P:a * N + (m + 1) * P],
+                                            rhs=moving[a][0].bitcast(FP8X4), rhs_scale=moving[a][1],
+                                            start=(a == 0), stop=(a == 2))
+                    if v0 + c0 + width == V and m == 1:
+                        nc.vector.tensor_copy(result[:, m, :], acc[:])
+                    else:
+                        nc.scalar.copy(result[:, m, :], acc[:])
+                nc.sync.dma_start(out_rows[:, :, v0 + c0:v0 + c0 + width], result[:])

from contextlib import ExitStack

import concourse.mybir as mybir
from concourse.masks import make_identity

K, T, S, V, H, N = 512, 4096, 1024, 512, 512, 256
D = 4
FLOPS = 2 * K * H * S + 3 * 2 * H * N * V

F32 = mybir.dt.float32
BF16 = mybir.dt.bfloat16
I32 = mybir.dt.int32
U32 = mybir.dt.uint32
U16 = mybir.dt.uint16
U8 = mybir.dt.uint8
FP8X4 = mybir.dt.float8_e4m3fn_x4
MAX = mybir.AluOpType.max
MIN = mybir.AluOpType.min
COPY = mybir.ActivationFunctionType.Copy

P = 128
PACK = 4
BANK = 512
NODE_HALF = S // 2
TGT_HALF = V // 2
LIST_ROWS = 16
W1_SPLIT = 64


def tile_picked_pna_none_e_kernel(tc, xT, w1, w2_words, w2_scales, w3_words, w3_scales, w4_words, w4_scales, offs, pos1, pos2, pos3, pos4, out):
    nc = tc.nc
    with ExitStack() as ctx:
        keep = ctx.enter_context(tc.tile_pool(name="keep", bufs=1))
        psum = ctx.enter_context(tc.psum_pool(name="psum", bufs=1))

        def quantize(values, name):
            width = values.shape[1] // PACK
            codes = keep.tile([P, width], U32, name=name + "_codes", align_bytes=64)
            scales = keep.tile([P, width], U8, name=name + "_scales", align_bytes=64)
            nc.vector.quantize_mx(out=codes[:].bitcast(FP8X4), scales=scales[:], in_=values)
            return codes, scales

        offs_sb = keep.tile([P, S // LIST_ROWS], U16, name="offs_sb")
        x_rows = xT.rearrange("(p j) w -> p j w", j=PACK)
        planes = [keep.tile([P, T], F32, name="x_plane%d" % j) for j in range(PACK)]
        for j in range(PACK):
            nc.sync.dma_start(planes[j][:], x_rows[:, j, :])
            if j == 0:
                nc.sync.dma_start(offs_sb[:], offs)
        w1_rows = w1.rearrange("(p j) c -> p j c", j=PACK)
        w1_spans = ((0, W1_SPLIT), (W1_SPLIT, P))
        w1_raw = [keep.tile([P, PACK, PACK * (m1 - m0)], F32, name="w1_raw%d" % m0) for m0, m1 in w1_spans]
        for raw, (m0, m1) in zip(w1_raw, w1_spans):
            nc.sync.dma_start(raw[:], w1_rows[:, :, PACK * m0:PACK * m1])
        pos_sb = [keep.tile([P, V // LIST_ROWS], U16, name="pos_sb%d" % d) for d in range(D)]
        for d, pos in enumerate((pos1, pos2, pos3, pos4)):
            nc.sync.dma_start(pos_sb[d][:], pos)
        w_codes = [keep.tile([P, N], U32, name="w_codes%d" % a, align_bytes=64) for a in range(3)]
        for a, words in enumerate((w2_words, w3_words, w4_words)):
            nc.sync.dma_start(w_codes[a][:].bitcast(I32), words[0].rearrange("p n t -> p (n t)").bitcast(I32))
        w_scales = keep.tile([P, 3 * N], U8, name="w_scales", align_bytes=64)
        nc.gpsimd.memset(w_scales[:], 0)
        for a, scale_rows in enumerate((w2_scales, w3_scales, w4_scales)):
            for q in range(4):
                nc.sync.dma_start(w_scales[32 * q:32 * q + 4, a * N:(a + 1) * N].bitcast(I32), scale_rows[0, 4 * q:4 * q + 4, :].bitcast(I32))
        ident = keep.tile([P, P], F32, name="ident")
        make_identity(nc, ident[:])

        picked = [keep.tile([P, NODE_HALF, PACK], BF16, name="picked%d" % n, align_bytes=64) for n in range(2)]
        cols = NODE_HALF // LIST_ROWS
        for j in range(PACK):
            for n in range(2):
                nc.vector.tensor_copy(picked[n][:, :, j], planes[j][:].indirect(offs_sb[:, n * cols:(n + 1) * cols]))
                if j == PACK - 1 and n == 0:
                    xa_codes, xa_scales = quantize(picked[0][:].rearrange("p n j -> p (n j)"), "xa")

        w1_first = keep.tile([P, P, PACK], BF16, name="w1_first", tag="w1_then_xb", align_bytes=64)
        w1_rest = keep.tile([P, PACK - 1, P, PACK], BF16, name="w1_rest", align_bytes=64)
        for raw, (m0, m1) in zip(w1_raw, w1_spans):
            dealt = raw[:].rearrange("p j (m t) -> p m j t", t=PACK)
            nc.scalar.copy(w1_first[:, m0:m1, :], dealt[:, :, :, 0])
            nc.scalar.copy(w1_rest[:, :, m0:m1, :].rearrange("p t m j -> p m j t"), dealt[:, :, :, 1:PACK])
        w10_codes, w10_scales = quantize(w1_first[:].rearrange("p m j -> p (m j)"), "w1_0")
        xb_codes = keep.tile([P, NODE_HALF], U32, name="xb_codes", tag="w1_then_xb", align_bytes=64)
        xb_scales = keep.tile([P, NODE_HALF], U8, name="xb_scales", align_bytes=64)
        quarter = NODE_HALF // 2
        for r in range(2):
            span = slice(r * quarter, (r + 1) * quarter)
            nc.vector.quantize_mx(out=xb_codes[:, span].bitcast(FP8X4), scales=xb_scales[:, span],
                                  in_=picked[1][:, span, :].rearrange("p n j -> p (n j)"))
        w1_q = [(w10_codes[:], w10_scales[:])]

        h0 = keep.tile([P, S], F32, name="h0")
        h1 = keep.tile([P, S], F32, name="h1")
        h23 = keep.tile([P, 2, S], F32, name="h23")
        h = [h0[:], h1[:], h23[:, 0, :], h23[:, 1, :]]
        pieces = [((0,), 0, NODE_HALF), ((0,), NODE_HALF, quarter), ((0,), NODE_HALF + quarter, quarter),
                  ((1,), 0, NODE_HALF), ((1,), NODE_HALF, NODE_HALF), ((2,), 0, NODE_HALF), ((3,), 0, NODE_HALF),
                  ((2, 3), NODE_HALF, quarter), ((2, 3), NODE_HALF + quarter, quarter)]
        banks = ["mx0", "mx1", "mx2", "mx3", "back0", "back1", "mx0", "sums0", "sums1"]
        for bank, (ts, n0, width) in zip(banks, pieces):
            if ts == (1,) and n0 == 0:
                codes, scales = quantize(w1_rest[:, 0].rearrange("p m j -> p (m j)"), "w1_1")
                w1_q.append((codes[:], scales[:]))
                codes, scales = quantize(w1_rest[:, 1:3].rearrange("p t m j -> p (t m j)"), "w1_23")
                w1_q.extend([(codes[:, i * P:(i + 1) * P], scales[:, i * P:(i + 1) * P]) for i in range(2)])
            acc = psum.tile([P, len(ts), width], F32, name="acc", tag=bank)
            codes, scales = (xa_codes, xa_scales) if n0 < NODE_HALF else (xb_codes, xb_scales)
            span = slice(n0 % NODE_HALF, n0 % NODE_HALF + width)
            for i, t in enumerate(ts):
                nc.tensor.matmul_mx(acc[:, i, :], lhsT=w1_q[t][0].bitcast(FP8X4), lhsT_scale=w1_q[t][1],
                                    rhs=codes[:, span].bitcast(FP8X4), rhs_scale=scales[:, span], start=True, stop=True)
            if len(ts) == 2:
                nc.scalar.copy(h23[:, :, n0:n0 + width], acc[:])
            elif n0 == NODE_HALF + quarter:
                nc.vector.tensor_copy(h[ts[0]][:, n0:n0 + width], acc[:, 0, :])
            else:
                nc.scalar.copy(h[ts[0]][:, n0:n0 + width], acc[:, 0, :])

        g = [keep.tile([P, PACK, V], F32, name="g%d" % d) for d in range(D)]
        rounded = [keep.tile([P, V, PACK], BF16, name="rounded%d" % d, align_bytes=64) for d in range(D - 1)]
        back = [psum.tile([P, 2, TGT_HALF], F32, name="back", tag="back%d" % v) for v in range(2)]
        mean = [keep.tile([P, TGT_HALF * PACK], BF16, name="mean%d" % v, align_bytes=64) for v in range(2)]

        def round_and_weave(dst, d, span):
            nc.scalar.copy(dst.rearrange("p (c i) t -> p c t i", i=4),
                           g[d][:, :, span].rearrange("p t (c i) -> p c t i", i=4))

        for u in range(2):
            sums = [psum.tile([P, 2, 2, P], F32, name="sums", tag=("mx%d" % (1 + v), "sums%d" % v)[u]) for v in range(2)]
            if u == 0:
                order = [(d, e) for e in range(2) for d in range(D)]
            else:
                order = [(d, e) for d in range(D) for e in range(2)]
            for i, (d, e) in enumerate(order):
                t = 2 * u + e
                nc.vector.tensor_copy(g[d][:, t, :], h[t].indirect(pos_sb[d][:]))
                for b in range(V // P):
                    nc.tensor.matmul(sums[b // 2][:, b % 2, e, :], lhsT=g[d][:, t, b * P:(b + 1) * P], rhs=ident[:],
                                     is_transpose=True, start=(i == 0 and b % 2 == 0), stop=(i == len(order) - 1 and b % 2 == 1))
                if t == PACK - 1 and d < D - 1:
                    round_and_weave(rounded[d][:], d, slice(0, V))
            for v in range(2):
                mean_t = keep.tile([P, 2, P, 2], BF16, name="mean_t", tag="mean_t%d_%d" % (u, v), align_bytes=64)
                nc.scalar.activation(mean_t[:], sums[v][:].rearrange("p b e c -> p b c e"), COPY, scale=1.0 / D)
                mean_words = mean_t[:].rearrange("p b c e -> p (b c e)").bitcast(F32)
                for b in range(2):
                    nc.tensor.transpose(back[v][:, u, b * P:(b + 1) * P], mean_words[:, b * P:(b + 1) * P], ident[:])
        last = []
        for v in range(2):
            tile = keep.tile([P, TGT_HALF, PACK], BF16, name="last", tag="mean_t1_%d" % v, align_bytes=64)
            round_and_weave(tile[:], D - 1, slice(v * TGT_HALF, (v + 1) * TGT_HALF))
            last.append(tile[:].rearrange("p v t -> p (v t)"))
            nc.scalar.copy(mean[v][:].bitcast(F32).rearrange("p (v u) -> p v u", u=2), back[v][:].rearrange("p u v -> p v u"))

        flat = [r[:].rearrange("p v t -> p (v t)") for r in rounded]
        hi, lo = flat[0], flat[0]
        for d in range(1, D - 1):
            hi_next = keep.tile([P, V * PACK], BF16, name="hi%d" % d, align_bytes=64)
            lo_next = keep.tile([P, V * PACK], BF16, name="lo%d" % d, align_bytes=64)
            nc.vector.tensor_tensor(hi_next[:], hi, flat[d], MAX)
            nc.vector.tensor_tensor(lo_next[:], lo, flat[d], MIN)
            hi, lo = hi_next[:], lo_next[:]

        out_rows = out.rearrange("(m p) v -> p m v", p=P)
        free_banks = ["mx0", "mx3", "mx1", "mx2", "sums0", "sums1"]
        for v in range(2):
            v0 = v * TGT_HALF
            largest = keep.tile([P, TGT_HALF * PACK], BF16, name="largest%d" % v, align_bytes=64)
            nc.vector.tensor_tensor(largest[:], hi[:, v0 * PACK:(v0 + TGT_HALF) * PACK], last[v], MAX)
            z1 = quantize(mean[v][:], "z1_%d" % v)
            width = TGT_HALF // (v + 1)
            starts = range(0, TGT_HALF, width)
            smallest = [keep.tile([P, width * PACK], BF16, name="smallest%d_%d" % (v, c0), align_bytes=64) for c0 in starts]
            z2 = None
            for tile, c0 in zip(smallest, starts):
                span = slice((v0 + c0) * PACK, (v0 + c0 + width) * PACK)
                nc.vector.tensor_tensor(tile[:], lo[:, span], last[v][:, c0 * PACK:(c0 + width) * PACK], MIN)
                if c0 == 0:
                    z2 = quantize(largest[:], "z2_%d" % v)
            for tile, c0 in zip(smallest, starts):
                z3 = quantize(tile[:], "z3_%d_%d" % (v, c0))
                moving = [(z1[0][:, c0:c0 + width], z1[1][:, c0:c0 + width]), (z2[0][:, c0:c0 + width], z2[1][:, c0:c0 + width]), (z3[0][:], z3[1][:])]
                result = keep.tile([P, N // P, width], F32, name="result%d_%d" % (v, c0))
                for m in range(N // P):
                    acc = psum.tile([P, width], F32, name="acc", tag=free_banks.pop(0))
                    for a in range(3):
                        nc.tensor.matmul_mx(acc[:], lhsT=w_codes[a][:, m * P:(m + 1) * P].bitcast(FP8X4),
                                            lhsT_scale=w_scales[:, a * N + m * P:a * N + (m + 1) * P],
                                            rhs=moving[a][0].bitcast(FP8X4), rhs_scale=moving[a][1],
                                            start=(a == 0), stop=(a == 2))
                    if v0 + c0 + width == V and m == 1:
                        nc.vector.tensor_copy(result[:, m, :], acc[:])
                    else:
                        nc.scalar.copy(result[:, m, :], acc[:])
                nc.sync.dma_start(out_rows[:, :, v0 + c0:v0 + c0 + width], result[:])
